import numpy as np
import ml_dtypes


def mxq(x, axis, fmt="e4m3"):
    dtype, down = {"e4m3": (ml_dtypes.float8_e4m3fn, 7), "e5m2": (ml_dtypes.float8_e5m2, 14)}[fmt]
    v = np.moveaxis(np.asarray(x, np.float32).astype(ml_dtypes.bfloat16).astype(np.float64), axis, -1)
    blocks = v.reshape(v.shape[:-1] + (-1, 32))
    amax = np.abs(blocks).max(-1, keepdims=True)
    byte = np.maximum(np.where(amax > 0, np.frexp(amax)[1] - 1 + 127, 0) - down, 1)
    scale = np.exp2(byte - 127.0)
    codes = (blocks / scale).astype(np.float32).astype(dtype).astype(np.float64)
    return np.moveaxis((codes * scale).reshape(v.shape), -1, axis)


WIDE = False


def mx_kscale(k):
    if not WIDE:
        return np.ones(k)
    levels = np.array([10, -10, 5, -5, 0])
    if k % 512:
        return np.exp2(np.random.permutation(np.resize(levels, k // 32))).repeat(32)
    a = np.empty((k // 512, 16))
    for p in range(k // 512):
        a[p, :8] = np.random.permutation(np.resize(levels, 8))
        for g in range(8):
            far = levels[np.abs(levels - a[p, g]) >= 10]
            a[p, g + 8] = far[np.random.randint(len(far))]
    return np.exp2(a.ravel()).repeat(32)


def f64(x):
    return np.asarray(x).astype(np.float64)


def striped(idx):
    return np.tile(idx.reshape(-1, 16).T, (8, 1)).astype(np.uint16)


def unstriped(offs):
    return offs[:16].T.reshape(-1).astype(np.int64)


def striped8(idx):
    return np.concatenate([x.reshape(-1, 16).T for x in idx]).astype(np.uint16)


def runs(offs, k):
    lists = np.stack([offs[16 * r : 16 * r + 16].T.reshape(-1) for r in range(8)]).astype(np.int64)
    return lists[np.arange(k) % 512 // 64]


def pack_weight(w):
    k, n = w.shape
    w = f64(np.asarray(w, np.float32).astype(ml_dtypes.bfloat16)).reshape(k // 32, 32, n)
    amax = np.abs(w).max(1)
    byte = np.clip(np.where(amax > 0, np.frexp(amax)[1] - 1 + 127 - 7, 1), 1, 254)
    scaled = (w * np.exp2(127.0 - byte)[:, None, :]).reshape(k, n).astype(np.float32)
    words = np.ascontiguousarray(scaled.reshape(k // 512, 128, 4, n).transpose(0, 1, 3, 2)).astype(ml_dtypes.float8_e4m3fn).view(np.uint8)
    return words, np.ascontiguousarray(byte.astype(np.uint8).reshape(k // 512, 16, n))


def unpack_weight(words, scales):
    g, p, n, _ = words.shape
    vals = np.ascontiguousarray(words).view(ml_dtypes.float8_e4m3fn).astype(np.float64) * np.repeat(np.exp2(scales.astype(np.float64) - 127.0), 8, axis=1)[..., None]
    return vals.transpose(0, 1, 3, 2).reshape(g * 512, n)


def sigmoid(v):
    return 1.0 / (1.0 + np.exp(-np.maximum(v, -700.0)))


K, T, S, G, H, W = 512, 1024, 256, 2048, 512, 128


def setup_inputs():
    n = np.random.standard_normal
    s = mx_kscale(K)[:, None]
    packed_xT = pack_weight(n((K, T)) * s)
    packed_dT = pack_weight(n((K, G)) / s)
    perm = np.random.permutation(S)
    return {
        "x_words": packed_xT[0],
        "x_scales": packed_xT[1],
        "d_words": packed_dT[0],
        "d_scales": packed_dT[1],
        "gs": (np.random.uniform(0.5, 1.5, (K, 1)) * s).astype(np.float32),
        "sl": np.random.uniform(1.0, 2.0, (H, 1)).astype(np.float32),
        "th": (0.5 * n((H, 1))).astype(np.float32),
        "offs": striped8(np.random.randint(0, T, (8, S))),
        "ci": striped(np.random.permutation(G)[:H]),
        "n1": striped(perm[:W]),
        "n2": striped(perm[W:]),
        "k1": striped8(np.random.randint(0, G, (8, H))),
        "n3": striped8(np.stack([np.random.permutation(S) for _ in range(8)])),
        "n4": striped8(np.stack([np.random.permutation(S) for _ in range(8)])),
    }


def reference(x_words, x_scales, d_words, d_scales, gs, sl, th, offs, ci, n1, n2, k1, n3, n4):
    d_k1 = unpack_weight(d_words, d_scales)[np.arange(K)[:, None], runs(k1, K)]
    d_ci = unpack_weight(d_words, d_scales)[:, unstriped(ci)]
    xq = unpack_weight(x_words, x_scales)[np.arange(K)[:, None], runs(offs, K)]
    s = 0.0625 * (d_ci.T @ xq)
    pa = s[:, unstriped(n1)]
    pb = s[:, unstriped(n2)]
    rb = np.maximum(pa, pb)
    ra = pa / (np.abs(pb) + 0.5)
    ds = np.zeros((H, S))
    ds[:, unstriped(n1)] = ra
    dt = ds.copy()
    dt[:, unstriped(n2)] = rb
    z = f64(gs) * dt
    h = 0.0625 * ((d_k1.T @ mxq(z, 0, "e4m3")))
    sg = sigmoid(f64(sl) * (h[np.arange(H)[:, None], runs(n3, H)] - f64(th)))
    st = h * sg
    return st - (0.5 * (st[np.arange(H)[:, None], runs(n4, H)]))

@@ -1,0 +1,228 @@
+from contextlib import ExitStack
+
+import concourse.mybir as mybir
+
+K, T, S, G, H, W = 512, 1024, 256, 2048, 512, 128
+FLOPS = 2 * (2 * K * H * S)
+
+F32 = mybir.dt.float32
+BF16 = mybir.dt.bfloat16
+I32 = mybir.dt.int32
+U32 = mybir.dt.uint32
+U16 = mybir.dt.uint16
+U8 = mybir.dt.uint8
+FP8X4 = mybir.dt.float8_e4m3fn_x4
+ALU = mybir.AluOpType
+ACT = mybir.ActivationFunctionType
+
+P = 128
+R = 4
+SHRINK = 2.0 ** -124
+
+
+def tile_picked_hwqratioehp_none_p_kernel(
+    tc, x_words, x_scales, d_words, d_scales, gs, sl, th, offs, ci, n1, n2, k1, n3, n4, out
+):
+    nc = tc.nc
+    with ExitStack() as ctx:
+        lists = ctx.enter_context(tc.tile_pool(name="lists", bufs=1))
+        sb = ctx.enter_context(tc.tile_pool(name="sb", bufs=1))
+        psum = ctx.enter_context(tc.psum_pool(name="psum", bufs=1))
+
+        def load_list(name, src):
+            held = lists.tile(list(src.shape), U16, name=name)
+            nc.sync.dma_start(held[:], src)
+            return held
+
+        def move_scale_rows(queue, plane, picked):
+            for q in range(4):
+                queue.dma_start(plane[32 * q : 32 * q + 4, :].bitcast(I32), picked[32 * q : 32 * q + 32 : 8, :].bitcast(I32))
+
+        xw_table = sb.tile([P, T], U32, name="xw_table", tag="third")
+        dw_table = sb.tile([P, G], U32, name="dw_table")
+        xs_table = sb.tile([P, T], U8, name="xs_table")
+        ds_table = sb.tile([P, G], U8, name="ds_table", tag="first", align_bytes=64)
+        plane1 = sb.tile([P, S + H], U8, name="plane1", align_bytes=64)
+        plane2 = sb.tile([P, H], U8, name="plane2", align_bytes=64)
+        nc.vector.memset(xs_table[:].bitcast(I32), 0)
+        nc.vector.memset(ds_table[:].bitcast(I32), 0)
+        nc.vector.memset(plane1[:].bitcast(I32), 0)
+        nc.vector.memset(plane2[:].bitcast(I32), 0)
+
+        nc.scalar.dma_start(xs_table[0:P:8, :].bitcast(I32), x_scales[0].bitcast(I32))
+        nc.scalar.dma_start(ds_table[0:P:8, :].bitcast(I32), d_scales[0].bitcast(I32))
+        offs_t = load_list("offs_t", offs)
+        ci_t = load_list("ci_t", ci)
+        k1_t = load_list("k1_t", k1)
+        n1_t = load_list("n1_t", n1)
+        nc.sync.dma_start(dw_table[:].bitcast(I32), d_words[0].rearrange("p n j -> p (n j)").bitcast(I32))
+        nc.sync.dma_start(xw_table[:].bitcast(I32), x_words[0].rearrange("p n j -> p (n j)").bitcast(I32))
+        n2_t = load_list("n2_t", n2)
+        n3_t = load_list("n3_t", n3)
+        n4_t = load_list("n4_t", n4)
+        gs_t = sb.tile([P, R], F32, name="gs_t")
+        sl_t = sb.tile([P, R], F32, name="sl_t")
+        th_t = sb.tile([P, R], F32, name="th_t")
+        for held, src in ((gs_t, gs), (sl_t, sl), (th_t, th)):
+            nc.gpsimd.dma_start(held[:], src.rearrange("(p t) o -> p (t o)", t=R))
+        bias = sb.tile([P, R], F32, name="bias")
+        sl_th = sb.tile([P, R], F32, name="sl_th")
+        nc.gpsimd.tensor_tensor(sl_th[:], sl_t[:], th_t[:], ALU.mult)
+        nc.gpsimd.tensor_scalar(bias[:], sl_th[:], -1.0, 0.0, ALU.mult, ALU.add)
+
+        picked1 = sb.tile([P, S + H], U8, name="picked1")
+        nc.vector.tensor_copy(picked1[:, 0:S], xs_table[:].indirect(offs_t[:]))
+        nc.vector.tensor_copy(picked1[:, S:].rearrange("p (t m) -> p m t", t=R), ds_table[:].indirect(ci_t[:]))
+        move_scale_rows(nc.scalar, plane1, picked1)
+
+        k1_bytes = sb.tile([P, H], U8, name="k1_bytes", tag="second")
+        nc.vector.tensor_copy(k1_bytes[:], ds_table[:].indirect(k1_t[:]))
+
+        words1 = sb.tile([P, H + S], U32, name="words1", tag="first", align_bytes=64)
+        ci_words = words1[:, 0:H]
+        x_picked = words1[:, H:]
+        nc.vector.tensor_copy(ci_words.rearrange("p (t m) -> p m t", t=R), dw_table[:].indirect(ci_t[:]))
+        nc.vector.tensor_copy(x_picked, xw_table[:].indirect(offs_t[:]))
+
+        k1_bytes_dealt = sb.tile([P, H], U8, name="k1_bytes_dealt", tag="third")
+        nc.vector.tensor_copy(k1_bytes_dealt[:].rearrange("p (t m) -> p m t", t=R), k1_bytes[:].rearrange("p (m t) -> p m t", t=R))
+        move_scale_rows(nc.sync, plane2, k1_bytes_dealt)
+
+        s_banks = [psum.tile([P, S], F32, name="s_bank%d" % t) for t in range(R)]
+        for t in range(R):
+            nc.tensor.matmul_mx(
+                out=s_banks[t][:],
+                lhsT=ci_words[:, t * P : (t + 1) * P].bitcast(FP8X4),
+                lhsT_scale=plane1[:, S + t * P : S + (t + 1) * P],
+                rhs=x_picked.bitcast(FP8X4),
+                rhs_scale=plane1[:, 0:S],
+                start=True,
+                stop=True,
+            )
+
+        s_rows = [sb.tile([P, S], F32, name="s_rows%d" % t) for t in range(R)]
+        h_wide = [sb.tile([P, 2 * S], F32, name="h_wide%d" % t) for t in range(R)]
+        st_wide = [sb.tile([P, 2 * S], F32, name="st_wide%d" % t) for t in range(R)]
+
+        def spare(wide):
+            return wide[:, S:].rearrange("p (a w) -> p a w", a=2)
+
+        pb = [spare(h_wide[0]), spare(h_wide[1])]
+        pa = [spare(h_wide[2]), spare(h_wide[3])]
+        rb = [spare(st_wide[0]), spare(st_wide[1])]
+        ra = [spare(st_wide[2]), spare(st_wide[3])]
+        size = sb.tile([P, R, W], F32, name="size")
+        den = sb.tile([P, R, W], F32, name="den")
+        prod = sb.tile([P, R // 2, W], F32, name="prod")
+        rec = sb.tile([P, R // 2, W], F32, name="rec")
+        inv = sb.tile([P, R, W], F32, name="inv")
+        dt_rows = [sb.tile([P, S], F32, name="dt_rows%d" % t) for t in range(R)]
+        z_bf = sb.tile([P, S, R], BF16, name="z_bf", align_bytes=64)
+
+        k1_words = sb.tile([P, H], U32, name="k1_words", tag="second")
+        k1_words_dealt = sb.tile([P, H], U32, name="k1_words_dealt", align_bytes=64)
+
+        def pair(u):
+            return slice(2 * u, 2 * u + 2)
+
+        def fetch(dst, entries, t):
+            nc.scalar.activation(dst[t // 2][:, t % 2, :], s_rows[t][:].indirect(entries[:]), ACT.Copy)
+
+        def denominators(u):
+            nc.vector.scalar_tensor_tensor(size[:, pair(u), :], pb[u], -1.0, pb[u], ALU.mult, ALU.max)
+            nc.vector.tensor_scalar(den[:, pair(u), :], size[:, pair(u), :], 0.5, SHRINK, ALU.add, ALU.mult)
+            nc.vector.scalar_tensor_tensor(prod[:, u, :], den[:, 2 * u, :], 1.0 / SHRINK, den[:, 2 * u + 1, :], ALU.mult, ALU.mult)
+            nc.vector.reciprocal(rec[:, u, :], prod[:, u, :])
+
+        def larger(u):
+            nc.vector.tensor_tensor(rb[u], pa[u], pb[u], ALU.max)
+
+        def quotients(u):
+            a, b = 2 * u, 2 * u + 1
+            nc.vector.tensor_tensor(inv[:, pair(u), :], den[:, pair(u), :], rec[:, u : u + 1, :].to_broadcast([P, 2, W]), ALU.mult)
+            nc.vector.tensor_tensor(ra[u][:, 0, :], pa[u][:, 0, :], inv[:, b, :], ALU.mult)
+            nc.vector.tensor_tensor(ra[u][:, 1, :], pa[u][:, 1, :], inv[:, a, :], ALU.mult)
+
+        def put_back(src, entries, t):
+            nc.scalar.activation(dt_rows[t][:].indirect(entries[:]), src[t // 2][:, t % 2, :], ACT.Copy)
+
+        def weigh(t, cols):
+            nc.vector.tensor_scalar(z_bf[:, cols, t], dt_rows[t][:, cols], gs_t[:, t : t + 1], None, ALU.mult)
+
+        for t in (0, 1):
+            nc.scalar.activation(s_rows[t][:], s_banks[t][:], ACT.Copy, scale=0.0625)
+        for t in (2, 3):
+            nc.vector.tensor_scalar(s_rows[t][:], s_banks[t][:], 0.0625, None, ALU.mult)
+        for t in range(R):
+            fetch(pb, n2_t, t)
+        for t in range(R):
+            fetch(pa, n1_t, t)
+        denominators(0)
+        larger(0)
+        denominators(1)
+        larger(1)
+        quotients(0)
+        quotients(1)
+        for t in range(R):
+            put_back(rb, n2_t, t)
+        for t in range(R):
+            put_back(ra, n1_t, t)
+        nc.vector.tensor_copy(k1_words[:], dw_table[:].indirect(k1_t[:]))
+        nc.vector.tensor_copy(
+            k1_words_dealt[:].bitcast(I32).rearrange("p (t m) -> p m t", t=R),
+            k1_words[:].bitcast(I32).rearrange("p (m t) -> p m t", t=R),
+        )
+
+        halves = [slice(0, S // 2), slice(S // 2, S)]
+        for t in range(R - 1):
+            weigh(t, slice(0, S))
+        for cols in halves:
+            weigh(R - 1, cols)
+        z_words = sb.tile([P, S], U32, name="z_words", align_bytes=64)
+        z_plane = sb.tile([P, S], U8, name="z_plane", align_bytes=64)
+        for cols in halves:
+            nc.vector.quantize_mx(
+                out=z_words[:, cols].bitcast(FP8X4),
+                scales=z_plane[:, cols],
+                in_=z_bf[:, cols, :].rearrange("p n t -> p (n t)"),
+            )
+
+        h_banks = [psum.tile([P, S], F32, name="h_bank%d" % t) for t in range(R)]
+        for t in range(R):
+            nc.tensor.matmul_mx(
+                out=h_banks[t][:],
+                lhsT=k1_words_dealt[:, t * P : (t + 1) * P].bitcast(FP8X4),
+                lhsT_scale=plane2[:, t * P : (t + 1) * P],
+                rhs=z_words[:].bitcast(FP8X4),
+                rhs_scale=z_plane[:],
+                start=True,
+                stop=True,
+            )
+
+        h_rows = [wide[:, 0:S] for wide in h_wide]
+        st_rows = [wide[:, 0:S] for wide in st_wide]
+        sg = sb.tile([P, R, S], F32, name="sg")
+        far = sb.tile([P, R, S], F32, name="far")
+        res = sb.tile([P, R, S], F32, name="res")
+        out_rows = out.rearrange("(p t) n -> p t n", t=R)
+
+        def gate(t):
+            nc.scalar.activation(
+                sg[:, t, :], h_wide[t][:].indirect(n3_t[:]), ACT.Sigmoid, bias=bias[:, t : t + 1], scale=sl_t[:, t : t + 1]
+            )
+            nc.vector.tensor_tensor(st_rows[t], h_rows[t], sg[:, t, :], ALU.mult)
+
+        def finish(t, cols):
+            entries = n4_t[:, cols.start // 16 : cols.stop // 16]
+            nc.scalar.activation(far[:, t, cols], st_wide[t][:].indirect(entries), ACT.Copy)
+            nc.vector.scalar_tensor_tensor(res[:, t, cols], far[:, t, cols], -0.5, st_rows[t][:, cols], ALU.mult, ALU.add)
+            nc.sync.dma_start(out_rows[:, t, cols], res[:, t, cols])
+
+        for t in range(R):
+            nc.vector.tensor_scalar(h_rows[t], h_banks[t][:], 0.0625, None, ALU.mult)
+        for t in range(R):
+            gate(t)
+        for t in range(R - 1):
+            finish(t, slice(0, S))
+        for cols in halves:
+            finish(R - 1, cols)

@@ -34,9 +34,9 @@ def tile_picked_hwqratioehp_none_p_kernel(
             nc.sync.dma_start(held[:], src)
             return held
 
-        def move_scale_rows(queue, plane, picked):
+        def move_scale_rows(queues, plane, picked):
             for q in range(4):
-                queue.dma_start(plane[32 * q : 32 * q + 4, :].bitcast(I32), picked[32 * q : 32 * q + 32 : 8, :].bitcast(I32))
+                queues[q % len(queues)].dma_start(plane[32 * q : 32 * q + 4, :].bitcast(I32), picked[32 * q : 32 * q + 32 : 8, :].bitcast(I32))
 
         xw_table = sb.tile([P, T], U32, name="xw_table", tag="third")
         dw_table = sb.tile([P, G], U32, name="dw_table")
@@ -44,20 +44,19 @@ def tile_picked_hwqratioehp_none_p_kernel(
         ds_table = sb.tile([P, G], U8, name="ds_table", tag="first", align_bytes=64)
         plane1 = sb.tile([P, S + H], U8, name="plane1", align_bytes=64)
         plane2 = sb.tile([P, H], U8, name="plane2", align_bytes=64)
-        nc.vector.memset(xs_table[:].bitcast(I32), 0)
-        nc.vector.memset(ds_table[:].bitcast(I32), 0)
         nc.vector.memset(plane1[:].bitcast(I32), 0)
         nc.vector.memset(plane2[:].bitcast(I32), 0)
 
-        nc.scalar.dma_start(xs_table[0:P:8, :].bitcast(I32), x_scales[0].bitcast(I32))
-        nc.scalar.dma_start(ds_table[0:P:8, :].bitcast(I32), d_scales[0].bitcast(I32))
+        for table, scales in ((xs_table, x_scales), (ds_table, d_scales)):
+            rows = scales[0].bitcast(I32)
+            nc.scalar.dma_start(table[:].bitcast(I32), rows.unsqueeze(1).to_broadcast([16, 8, rows.shape[1]]))
         offs_t = load_list("offs_t", offs)
         ci_t = load_list("ci_t", ci)
         k1_t = load_list("k1_t", k1)
+        n2_t = load_list("n2_t", n2)
         n1_t = load_list("n1_t", n1)
         nc.sync.dma_start(dw_table[:].bitcast(I32), d_words[0].rearrange("p n j -> p (n j)").bitcast(I32))
         nc.sync.dma_start(xw_table[:].bitcast(I32), x_words[0].rearrange("p n j -> p (n j)").bitcast(I32))
-        n2_t = load_list("n2_t", n2)
         n3_t = load_list("n3_t", n3)
         n4_t = load_list("n4_t", n4)
         gs_t = sb.tile([P, R], F32, name="gs_t")
@@ -73,7 +72,7 @@ def tile_picked_hwqratioehp_none_p_kernel(
         picked1 = sb.tile([P, S + H], U8, name="picked1")
         nc.vector.tensor_copy(picked1[:, 0:S], xs_table[:].indirect(offs_t[:]))
         nc.vector.tensor_copy(picked1[:, S:].rearrange("p (t m) -> p m t", t=R), ds_table[:].indirect(ci_t[:]))
-        move_scale_rows(nc.scalar, plane1, picked1)
+        move_scale_rows([nc.scalar, nc.sync], plane1, picked1)
 
         k1_bytes = sb.tile([P, H], U8, name="k1_bytes", tag="second")
         nc.vector.tensor_copy(k1_bytes[:], ds_table[:].indirect(k1_t[:]))
@@ -86,9 +85,9 @@ def tile_picked_hwqratioehp_none_p_kernel(
 
         k1_bytes_dealt = sb.tile([P, H], U8, name="k1_bytes_dealt", tag="third")
         nc.vector.tensor_copy(k1_bytes_dealt[:].rearrange("p (t m) -> p m t", t=R), k1_bytes[:].rearrange("p (m t) -> p m t", t=R))
-        move_scale_rows(nc.sync, plane2, k1_bytes_dealt)
+        move_scale_rows([nc.sync], plane2, k1_bytes_dealt)
 
-        s_banks = [psum.tile([P, S], F32, name="s_bank%d" % t) for t in range(R)]
+        s_banks = [psum.tile([P, S], F32, name="s_bank%d" % t, tag="bank%d" % t) for t in range(R)]
         for t in range(R):
             nc.tensor.matmul_mx(
                 out=s_banks[t][:],
@@ -115,9 +114,8 @@ def tile_picked_hwqratioehp_none_p_kernel(
         den = sb.tile([P, R, W], F32, name="den")
         prod = sb.tile([P, R // 2, W], F32, name="prod")
         rec = sb.tile([P, R // 2, W], F32, name="rec")
-        inv = sb.tile([P, R, W], F32, name="inv")
+        inv = sb.tile([P, R, W], F32, name="inv", tag="fourth", align_bytes=64)
         dt_rows = [sb.tile([P, S], F32, name="dt_rows%d" % t) for t in range(R)]
-        z_bf = sb.tile([P, S, R], BF16, name="z_bf", align_bytes=64)
 
         k1_words = sb.tile([P, H], U32, name="k1_words", tag="second")
         k1_words_dealt = sb.tile([P, H], U32, name="k1_words_dealt", align_bytes=64)
@@ -149,29 +147,30 @@ def tile_picked_hwqratioehp_none_p_kernel(
         def weigh(t, cols):
             nc.vector.tensor_scalar(z_bf[:, cols, t], dt_rows[t][:, cols], gs_t[:, t : t + 1], None, ALU.mult)
 
+        nc.vector.tensor_copy(k1_words[:], dw_table[:].indirect(k1_t[:]))
+        nc.vector.tensor_copy(
+            k1_words_dealt[:].bitcast(I32).rearrange("p (t m) -> p m t", t=R),
+            k1_words[:].bitcast(I32).rearrange("p (m t) -> p m t", t=R),
+        )
         for t in (0, 1):
             nc.scalar.activation(s_rows[t][:], s_banks[t][:], ACT.Copy, scale=0.0625)
         for t in (2, 3):
             nc.vector.tensor_scalar(s_rows[t][:], s_banks[t][:], 0.0625, None, ALU.mult)
-        for t in range(R):
-            fetch(pb, n2_t, t)
-        for t in range(R):
-            fetch(pa, n1_t, t)
-        denominators(0)
+        for u in range(R // 2):
+            for dst, entries in ((pb, n2_t), (pa, n1_t)):
+                for t in (2 * u, 2 * u + 1):
+                    fetch(dst, entries, t)
         larger(0)
-        denominators(1)
         larger(1)
+        denominators(0)
+        denominators(1)
         quotients(0)
         quotients(1)
         for t in range(R):
             put_back(rb, n2_t, t)
         for t in range(R):
             put_back(ra, n1_t, t)
-        nc.vector.tensor_copy(k1_words[:], dw_table[:].indirect(k1_t[:]))
-        nc.vector.tensor_copy(
-            k1_words_dealt[:].bitcast(I32).rearrange("p (t m) -> p m t", t=R),
-            k1_words[:].bitcast(I32).rearrange("p (m t) -> p m t", t=R),
-        )
+        z_bf = sb.tile([P, S, R], BF16, name="z_bf", tag="fourth", align_bytes=64)
 
         halves = [slice(0, S // 2), slice(S // 2, S)]
         for t in range(R - 1):
@@ -187,14 +186,17 @@ def tile_picked_hwqratioehp_none_p_kernel(
                 in_=z_bf[:, cols, :].rearrange("p n t -> p (n t)"),
             )
 
-        h_banks = [psum.tile([P, S], F32, name="h_bank%d" % t) for t in range(R)]
-        for t in range(R):
+        pieces = [(0, cols) for cols in halves] + [(t, slice(0, S)) for t in range(1, R)]
+        h_banks = []
+        for i, (t, cols) in enumerate(pieces):
+            bank = psum.tile([P, cols.stop - cols.start], F32, name="h_bank%d" % i, tag="bank%d" % ((R + i) % 8))
+            h_banks.append(bank)
             nc.tensor.matmul_mx(
-                out=h_banks[t][:],
+                out=bank[:],
                 lhsT=k1_words_dealt[:, t * P : (t + 1) * P].bitcast(FP8X4),
                 lhsT_scale=plane2[:, t * P : (t + 1) * P],
-                rhs=z_words[:].bitcast(FP8X4),
-                rhs_scale=z_plane[:],
+                rhs=z_words[:, cols].bitcast(FP8X4),
+                rhs_scale=z_plane[:, cols],
                 start=True,
                 stop=True,
             )
@@ -218,8 +220,8 @@ def tile_picked_hwqratioehp_none_p_kernel(
             nc.vector.scalar_tensor_tensor(res[:, t, cols], far[:, t, cols], -0.5, st_rows[t][:, cols], ALU.mult, ALU.add)
             nc.sync.dma_start(out_rows[:, t, cols], res[:, t, cols])
 
-        for t in range(R):
-            nc.vector.tensor_scalar(h_rows[t], h_banks[t][:], 0.0625, None, ALU.mult)
+        for bank, (t, cols) in zip(h_banks, pieces):
+            nc.vector.tensor_scalar(h_rows[t][:, cols], bank[:], 0.0625, None, ALU.mult)
         for t in range(R):
             gate(t)
         for t in range(R - 1):

@@ -47,6 +47,9 @@ def tile_picked_hwqratioehp_none_p_kernel(
         nc.vector.memset(plane1[:].bitcast(I32), 0)
         nc.vector.memset(plane2[:].bitcast(I32), 0)
 
+        warm = sb.tile([P, 2], F32, name="warm")
+        nc.vector.memset(warm[:, 0:1], 0.0)
+        nc.scalar.activation(warm[:, 1:2], warm[:, 0:1], ACT.Sigmoid)
         for table, scales in ((xs_table, x_scales), (ds_table, d_scales)):
             rows = scales[0].bitcast(I32)
             nc.scalar.dma_start(table[:].bitcast(I32), rows.unsqueeze(1).to_broadcast([16, 8, rows.shape[1]]))

@@ -50,10 +50,13 @@ def tile_picked_hwqratioehp_none_p_kernel(
         warm = sb.tile([P, 2], F32, name="warm")
         nc.vector.memset(warm[:, 0:1], 0.0)
         nc.scalar.activation(warm[:, 1:2], warm[:, 0:1], ACT.Sigmoid)
-        for table, scales in ((xs_table, x_scales), (ds_table, d_scales)):
+        def load_scales(table, scales):
             rows = scales[0].bitcast(I32)
-            nc.scalar.dma_start(table[:].bitcast(I32), rows.unsqueeze(1).to_broadcast([16, 8, rows.shape[1]]))
+            nc.sync.dma_start(table[:].bitcast(I32), rows.unsqueeze(1).to_broadcast([16, 8, rows.shape[1]]))
+
+        load_scales(xs_table, x_scales)
         offs_t = load_list("offs_t", offs)
+        load_scales(ds_table, d_scales)
         ci_t = load_list("ci_t", ci)
         k1_t = load_list("k1_t", k1)
         n2_t = load_list("n2_t", n2)
@@ -87,7 +90,7 @@ def tile_picked_hwqratioehp_none_p_kernel(
         nc.vector.tensor_copy(x_picked, xw_table[:].indirect(offs_t[:]))
 
         k1_bytes_dealt = sb.tile([P, H], U8, name="k1_bytes_dealt", tag="third")
-        nc.vector.tensor_copy(k1_bytes_dealt[:].rearrange("p (t m) -> p m t", t=R), k1_bytes[:].rearrange("p (m t) -> p m t", t=R))
+        nc.vector.tensor_copy(k1_bytes_dealt[:].rearrange("p (t a m) -> p a t m", t=R, m=16), k1_bytes[:].rearrange("p (a m t) -> p a t m", t=R, m=16))
         move_scale_rows([nc.sync], plane2, k1_bytes_dealt)
 
         s_banks = [psum.tile([P, S], F32, name="s_bank%d" % t, tag="bank%d" % t) for t in range(R)]
@@ -152,8 +155,8 @@ def tile_picked_hwqratioehp_none_p_kernel(
 
         nc.vector.tensor_copy(k1_words[:], dw_table[:].indirect(k1_t[:]))
         nc.vector.tensor_copy(
-            k1_words_dealt[:].bitcast(I32).rearrange("p (t m) -> p m t", t=R),
-            k1_words[:].bitcast(I32).rearrange("p (m t) -> p m t", t=R),
+            k1_words_dealt[:].bitcast(I32).rearrange("p (t a m) -> p a t m", t=R, m=4),
+            k1_words[:].bitcast(I32).rearrange("p (a m t) -> p a t m", t=R, m=4),
         )
         for t in (0, 1):
             nc.scalar.activation(s_rows[t][:], s_banks[t][:], ACT.Copy, scale=0.0625)

@@ -136,16 +136,15 @@ def tile_picked_hwqratioehp_none_p_kernel(
             nc.vector.scalar_tensor_tensor(size[:, pair(u), :], pb[u], -1.0, pb[u], ALU.mult, ALU.max)
             nc.vector.tensor_scalar(den[:, pair(u), :], size[:, pair(u), :], 0.5, SHRINK, ALU.add, ALU.mult)
             nc.vector.scalar_tensor_tensor(prod[:, u, :], den[:, 2 * u, :], 1.0 / SHRINK, den[:, 2 * u + 1, :], ALU.mult, ALU.mult)
-            nc.vector.reciprocal(rec[:, u, :], prod[:, u, :])
 
         def larger(u):
             nc.vector.tensor_tensor(rb[u], pa[u], pb[u], ALU.max)
 
-        def quotients(u):
+        def quotients(u, engine):
             a, b = 2 * u, 2 * u + 1
-            nc.vector.tensor_tensor(inv[:, pair(u), :], den[:, pair(u), :], rec[:, u : u + 1, :].to_broadcast([P, 2, W]), ALU.mult)
-            nc.vector.tensor_tensor(ra[u][:, 0, :], pa[u][:, 0, :], inv[:, b, :], ALU.mult)
-            nc.vector.tensor_tensor(ra[u][:, 1, :], pa[u][:, 1, :], inv[:, a, :], ALU.mult)
+            engine.tensor_tensor(inv[:, pair(u), :], den[:, pair(u), :], rec[:, u : u + 1, :].to_broadcast([P, 2, W]), ALU.mult)
+            engine.tensor_tensor(ra[u][:, 0, :], pa[u][:, 0, :], inv[:, b, :], ALU.mult)
+            engine.tensor_tensor(ra[u][:, 1, :], pa[u][:, 1, :], inv[:, a, :], ALU.mult)
 
         def put_back(src, entries, t):
             nc.scalar.activation(dt_rows[t][:].indirect(entries[:]), src[t // 2][:, t % 2, :], ACT.Copy)
@@ -170,8 +169,10 @@ def tile_picked_hwqratioehp_none_p_kernel(
         larger(1)
         denominators(0)
         denominators(1)
-        quotients(0)
-        quotients(1)
+        for u in range(R // 2):
+            nc.vector.reciprocal(rec[:, u, :], prod[:, u, :])
+        quotients(0, nc.gpsimd)
+        quotients(1, nc.vector)
         for t in range(R):
             put_back(rb, n2_t, t)
         for t in range(R):

from contextlib import ExitStack

import concourse.mybir as mybir

K, T, S, G, H, W = 512, 1024, 256, 2048, 512, 128
FLOPS = 2 * (2 * K * H * S)

F32 = mybir.dt.float32
BF16 = mybir.dt.bfloat16
I32 = mybir.dt.int32
U32 = mybir.dt.uint32
U16 = mybir.dt.uint16
U8 = mybir.dt.uint8
FP8X4 = mybir.dt.float8_e4m3fn_x4
ALU = mybir.AluOpType
ACT = mybir.ActivationFunctionType

P = 128
R = 4
SHRINK = 2.0 ** -124


def tile_picked_hwqratioehp_none_p_kernel(
    tc, x_words, x_scales, d_words, d_scales, gs, sl, th, offs, ci, n1, n2, k1, n3, n4, out
):
    nc = tc.nc
    with ExitStack() as ctx:
        lists = ctx.enter_context(tc.tile_pool(name="lists", bufs=1))
        sb = ctx.enter_context(tc.tile_pool(name="sb", bufs=1))
        psum = ctx.enter_context(tc.psum_pool(name="psum", bufs=1))

        def load_list(name, src):
            held = lists.tile(list(src.shape), U16, name=name)
            nc.sync.dma_start(held[:], src)
            return held

        def move_scale_rows(queues, plane, picked):
            for q in range(4):
                queues[q % len(queues)].dma_start(plane[32 * q : 32 * q + 4, :].bitcast(I32), picked[32 * q : 32 * q + 32 : 8, :].bitcast(I32))

        xw_table = sb.tile([P, T], U32, name="xw_table", tag="third")
        dw_table = sb.tile([P, G], U32, name="dw_table")
        xs_table = sb.tile([P, T], U8, name="xs_table")
        ds_table = sb.tile([P, G], U8, name="ds_table", tag="first", align_bytes=64)
        plane1 = sb.tile([P, S + H], U8, name="plane1", align_bytes=64)
        plane2 = sb.tile([P, H], U8, name="plane2", align_bytes=64)
        nc.vector.memset(plane1[:].bitcast(I32), 0)
        nc.vector.memset(plane2[:].bitcast(I32), 0)

        warm = sb.tile([P, 2], F32, name="warm")
        nc.vector.memset(warm[:, 0:1], 0.0)
        nc.scalar.activation(warm[:, 1:2], warm[:, 0:1], ACT.Sigmoid)
        def load_scales(table, scales):
            rows = scales[0].bitcast(I32)
            nc.sync.dma_start(table[:].bitcast(I32), rows.unsqueeze(1).to_broadcast([16, 8, rows.shape[1]]))

        load_scales(xs_table, x_scales)
        offs_t = load_list("offs_t", offs)
        load_scales(ds_table, d_scales)
        ci_t = load_list("ci_t", ci)
        k1_t = load_list("k1_t", k1)
        n2_t = load_list("n2_t", n2)
        n1_t = load_list("n1_t", n1)
        nc.sync.dma_start(dw_table[:].bitcast(I32), d_words[0].rearrange("p n j -> p (n j)").bitcast(I32))
        nc.sync.dma_start(xw_table[:].bitcast(I32), x_words[0].rearrange("p n j -> p (n j)").bitcast(I32))
        n3_t = load_list("n3_t", n3)
        n4_t = load_list("n4_t", n4)
        gs_t = sb.tile([P, R], F32, name="gs_t")
        sl_t = sb.tile([P, R], F32, name="sl_t")
        th_t = sb.tile([P, R], F32, name="th_t")
        for held, src in ((gs_t, gs), (sl_t, sl), (th_t, th)):
            nc.gpsimd.dma_start(held[:], src.rearrange("(p t) o -> p (t o)", t=R))
        bias = sb.tile([P, R], F32, name="bias")
        sl_th = sb.tile([P, R], F32, name="sl_th")
        nc.gpsimd.tensor_tensor(sl_th[:], sl_t[:], th_t[:], ALU.mult)
        nc.gpsimd.tensor_scalar(bias[:], sl_th[:], -1.0, 0.0, ALU.mult, ALU.add)

        picked1 = sb.tile([P, S + H], U8, name="picked1")
        nc.vector.tensor_copy(picked1[:, 0:S], xs_table[:].indirect(offs_t[:]))
        nc.vector.tensor_copy(picked1[:, S:].rearrange("p (t m) -> p m t", t=R), ds_table[:].indirect(ci_t[:]))
        move_scale_rows([nc.scalar, nc.sync], plane1, picked1)

        k1_bytes = sb.tile([P, H], U8, name="k1_bytes", tag="second")
        nc.vector.tensor_copy(k1_bytes[:], ds_table[:].indirect(k1_t[:]))

        words1 = sb.tile([P, H + S], U32, name="words1", tag="first", align_bytes=64)
        ci_words = words1[:, 0:H]
        x_picked = words1[:, H:]
        nc.vector.tensor_copy(ci_words.rearrange("p (t m) -> p m t", t=R), dw_table[:].indirect(ci_t[:]))
        nc.vector.tensor_copy(x_picked, xw_table[:].indirect(offs_t[:]))

        k1_bytes_dealt = sb.tile([P, H], U8, name="k1_bytes_dealt", tag="third")
        nc.vector.tensor_copy(k1_bytes_dealt[:].rearrange("p (t a m) -> p a t m", t=R, m=16), k1_bytes[:].rearrange("p (a m t) -> p a t m", t=R, m=16))
        move_scale_rows([nc.sync], plane2, k1_bytes_dealt)

        s_banks = [psum.tile([P, S], F32, name="s_bank%d" % t, tag="bank%d" % t) for t in range(R)]
        for t in range(R):
            nc.tensor.matmul_mx(
                out=s_banks[t][:],
                lhsT=ci_words[:, t * P : (t + 1) * P].bitcast(FP8X4),
                lhsT_scale=plane1[:, S + t * P : S + (t + 1) * P],
                rhs=x_picked.bitcast(FP8X4),
                rhs_scale=plane1[:, 0:S],
                start=True,
                stop=True,
            )

        s_rows = [sb.tile([P, S], F32, name="s_rows%d" % t) for t in range(R)]
        h_wide = [sb.tile([P, 2 * S], F32, name="h_wide%d" % t) for t in range(R)]
        st_wide = [sb.tile([P, 2 * S], F32, name="st_wide%d" % t) for t in range(R)]

        def spare(wide):
            return wide[:, S:].rearrange("p (a w) -> p a w", a=2)

        pb = [spare(h_wide[0]), spare(h_wide[1])]
        pa = [spare(h_wide[2]), spare(h_wide[3])]
        rb = [spare(st_wide[0]), spare(st_wide[1])]
        ra = [spare(st_wide[2]), spare(st_wide[3])]
        size = sb.tile([P, R, W], F32, name="size")
        den = sb.tile([P, R, W], F32, name="den")
        prod = sb.tile([P, R // 2, W], F32, name="prod")
        rec = sb.tile([P, R // 2, W], F32, name="rec")
        inv = sb.tile([P, R, W], F32, name="inv", tag="fourth", align_bytes=64)
        dt_rows = [sb.tile([P, S], F32, name="dt_rows%d" % t) for t in range(R)]

        k1_words = sb.tile([P, H], U32, name="k1_words", tag="second")
        k1_words_dealt = sb.tile([P, H], U32, name="k1_words_dealt", align_bytes=64)

        def pair(u):
            return slice(2 * u, 2 * u + 2)

        def fetch(dst, entries, t):
            nc.scalar.activation(dst[t // 2][:, t % 2, :], s_rows[t][:].indirect(entries[:]), ACT.Copy)

        def denominators(u):
            nc.vector.scalar_tensor_tensor(size[:, pair(u), :], pb[u], -1.0, pb[u], ALU.mult, ALU.max)
            nc.vector.tensor_scalar(den[:, pair(u), :], size[:, pair(u), :], 0.5, SHRINK, ALU.add, ALU.mult)
            nc.vector.scalar_tensor_tensor(prod[:, u, :], den[:, 2 * u, :], 1.0 / SHRINK, den[:, 2 * u + 1, :], ALU.mult, ALU.mult)

        def larger(u):
            nc.vector.tensor_tensor(rb[u], pa[u], pb[u], ALU.max)

        def quotients(u, engine):
            a, b = 2 * u, 2 * u + 1
            engine.tensor_tensor(inv[:, pair(u), :], den[:, pair(u), :], rec[:, u : u + 1, :].to_broadcast([P, 2, W]), ALU.mult)
            engine.tensor_tensor(ra[u][:, 0, :], pa[u][:, 0, :], inv[:, b, :], ALU.mult)
            engine.tensor_tensor(ra[u][:, 1, :], pa[u][:, 1, :], inv[:, a, :], ALU.mult)

        def put_back(src, entries, t):
            nc.scalar.activation(dt_rows[t][:].indirect(entries[:]), src[t // 2][:, t % 2, :], ACT.Copy)

        def weigh(t, cols):
            nc.vector.tensor_scalar(z_bf[:, cols, t], dt_rows[t][:, cols], gs_t[:, t : t + 1], None, ALU.mult)

        nc.vector.tensor_copy(k1_words[:], dw_table[:].indirect(k1_t[:]))
        nc.vector.tensor_copy(
            k1_words_dealt[:].bitcast(I32).rearrange("p (t a m) -> p a t m", t=R, m=4),
            k1_words[:].bitcast(I32).rearrange("p (a m t) -> p a t m", t=R, m=4),
        )
        for t in (0, 1):
            nc.scalar.activation(s_rows[t][:], s_banks[t][:], ACT.Copy, scale=0.0625)
        for t in (2, 3):
            nc.vector.tensor_scalar(s_rows[t][:], s_banks[t][:], 0.0625, None, ALU.mult)
        for u in range(R // 2):
            for dst, entries in ((pb, n2_t), (pa, n1_t)):
                for t in (2 * u, 2 * u + 1):
                    fetch(dst, entries, t)
        larger(0)
        larger(1)
        denominators(0)
        denominators(1)
        for u in range(R // 2):
            nc.vector.reciprocal(rec[:, u, :], prod[:, u, :])
        quotients(0, nc.gpsimd)
        quotients(1, nc.vector)
        for t in range(R):
            put_back(rb, n2_t, t)
        for t in range(R):
            put_back(ra, n1_t, t)
        z_bf = sb.tile([P, S, R], BF16, name="z_bf", tag="fourth", align_bytes=64)

        halves = [slice(0, S // 2), slice(S // 2, S)]
        for t in range(R - 1):
            weigh(t, slice(0, S))
        for cols in halves:
            weigh(R - 1, cols)
        z_words = sb.tile([P, S], U32, name="z_words", align_bytes=64)
        z_plane = sb.tile([P, S], U8, name="z_plane", align_bytes=64)
        for cols in halves:
            nc.vector.quantize_mx(
                out=z_words[:, cols].bitcast(FP8X4),
                scales=z_plane[:, cols],
                in_=z_bf[:, cols, :].rearrange("p n t -> p (n t)"),
            )

        pieces = [(0, cols) for cols in halves] + [(t, slice(0, S)) for t in range(1, R)]
        h_banks = []
        for i, (t, cols) in enumerate(pieces):
            bank = psum.tile([P, cols.stop - cols.start], F32, name="h_bank%d" % i, tag="bank%d" % ((R + i) % 8))
            h_banks.append(bank)
            nc.tensor.matmul_mx(
                out=bank[:],
                lhsT=k1_words_dealt[:, t * P : (t + 1) * P].bitcast(FP8X4),
                lhsT_scale=plane2[:, t * P : (t + 1) * P],
                rhs=z_words[:, cols].bitcast(FP8X4),
                rhs_scale=z_plane[:, cols],
                start=True,
                stop=True,
            )

        h_rows = [wide[:, 0:S] for wide in h_wide]
        st_rows = [wide[:, 0:S] for wide in st_wide]
        sg = sb.tile([P, R, S], F32, name="sg")
        far = sb.tile([P, R, S], F32, name="far")
        res = sb.tile([P, R, S], F32, name="res")
        out_rows = out.rearrange("(p t) n -> p t n", t=R)

        def gate(t):
            nc.scalar.activation(
                sg[:, t, :], h_wide[t][:].indirect(n3_t[:]), ACT.Sigmoid, bias=bias[:, t : t + 1], scale=sl_t[:, t : t + 1]
            )
            nc.vector.tensor_tensor(st_rows[t], h_rows[t], sg[:, t, :], ALU.mult)

        def finish(t, cols):
            entries = n4_t[:, cols.start // 16 : cols.stop // 16]
            nc.scalar.activation(far[:, t, cols], st_wide[t][:].indirect(entries), ACT.Copy)
            nc.vector.scalar_tensor_tensor(res[:, t, cols], far[:, t, cols], -0.5, st_rows[t][:, cols], ALU.mult, ALU.add)
            nc.sync.dma_start(out_rows[:, t, cols], res[:, t, cols])

        for bank, (t, cols) in zip(h_banks, pieces):
            nc.vector.tensor_scalar(h_rows[t][:, cols], bank[:], 0.0625, None, ALU.mult)
        for t in range(R):
            gate(t)
        for t in range(R - 1):
            finish(t, slice(0, S))
        for cols in halves:
            finish(R - 1, cols)
